import numpy as np
CORES = [67,68,75,76,83,84,91,92,99,100,107,108,115,116,123,124]
N = 16
ROOT = 0
WIDTHS = [256,256,5,128,256,128,256,256,5,256,5,5,256,25,256,25]
XW = 256
def setup_inputs(rng):
    return {"x": rng.standard_normal((N, 128, XW), dtype=np.float32)}
def reference(x):
    g = np.concatenate([x[r][:, :WIDTHS[r]] for r in range(N)], axis=1)
    y = np.full((N, 128, g.shape[1]), np.nan, x.dtype)
    y[ROOT] = g
    return {"y": y}

@@ -1,0 +1,118 @@
+TOTAL = 2374
+MIN_STORE = 64
+N_IN = 4
+N_ARR = 8
+
+SCRATCH = {
+    "land": ("sbuf", [128, TOTAL], "float32"),
+}
+SEMAPHORES = ["loaded", "sent", "stored"] + ["in%d" % k for k in range(N_IN)] + ["a%d" % k for k in range(N_ARR)]
+
+
+def engines(topo, src, dst):
+    return bin(topo.mask(src, dst)).count("1")
+
+
+def make_plan(T, topo):
+    widths = T.tables["WIDTHS"]
+    cores = list(T.cores)
+    root_rank = T.root if T.root is not None else 0
+    root = cores[root_rank]
+    off = [sum(widths[:r]) for r in range(len(widths) + 1)]
+    others = [r for r in range(len(cores)) if r != root_rank]
+
+    blocks = []
+    for r in others:
+        new_chip = not blocks or topo.chip(cores[blocks[-1][-1]]) != topo.chip(cores[r])
+        adjacent = bool(blocks) and blocks[-1][-1] == r - 1
+        chip_width = sum(widths[q] for q in others if topo.chip(cores[q]) == topo.chip(cores[r]))
+        if blocks and adjacent and (not new_chip or chip_width < MIN_STORE):
+            blocks[-1].append(r)
+        else:
+            blocks.append([r])
+    block_of = {r: b for b, rs in enumerate(blocks) for r in rs}
+
+    mate_chip = topo.chip(root) ^ 1
+    relays = [c for c in range(mate_chip * 8, mate_chip * 8 + 8) if topo.may_write(c, root)]
+    die_load = {0: 0, 1: 0}
+    core_load = {c: 0 for c in relays}
+    holder = {}
+    relayed = []
+    for r in others:
+        c = cores[r]
+        same_parity = (topo.chip(c) & 1) == (topo.chip(root) & 1)
+        if same_parity or (topo.chip(c) == mate_chip and topo.may_write(c, root)):
+            holder[r] = c
+            if not same_parity:
+                die_load[topo.die(c)] += widths[r]
+                core_load[c] += widths[r]
+        else:
+            relayed.append(r)
+    for r in sorted(relayed, key=lambda q: (-widths[q], q)):
+        c = min(relays, key=lambda k: (die_load[topo.die(k)], core_load[k], k))
+        holder[r] = c
+        die_load[topo.die(c)] += widths[r]
+        core_load[c] += widths[r]
+
+    sends = {}
+    arrive = [0] * len(blocks)
+    depth = [1] * len(blocks)
+    for h in sorted(set(holder.values())):
+        groups = []
+        for r in sorted(q for q in others if holder[q] == h):
+            if groups and groups[-1][-1] == r - 1 and block_of[groups[-1][-1]] == block_of[r]:
+                groups[-1].append(r)
+            else:
+                groups.append([r])
+        groups.sort(key=lambda rs: (off[rs[-1] + 1] - off[rs[0]], rs[0]))
+        k = 0
+        for rs in groups:
+            guests = [r for r in rs if cores[r] != h]
+            wait = None
+            if guests:
+                wait = ("in%d" % k, sum(engines(topo, cores[r], h) for r in guests))
+                for r in guests:
+                    sends.setdefault(cores[r], []).append(
+                        {"c0": off[r], "c1": off[r + 1], "dst": h, "sem": "in%d" % k, "wait": None})
+                k += 1
+                depth[block_of[rs[0]]] = 2
+            sends.setdefault(h, []).append(
+                {"c0": off[rs[0]], "c1": off[rs[-1] + 1], "dst": root, "sem": "a%d" % block_of[rs[0]], "wait": wait})
+            arrive[block_of[rs[0]]] += engines(topo, h, root)
+
+    stores = [{"c0": off[rs[0]], "c1": off[rs[-1] + 1], "sem": "a%d" % b, "count": arrive[b], "depth": depth[b]}
+              for b, rs in enumerate(blocks)]
+    stores.sort(key=lambda s: (s["depth"], s["c1"] - s["c0"], s["c0"]))
+    return {"root": root, "root_rank": root_rank, "off": off, "widths": widths, "sends": sends, "stores": stores}
+
+
+def rank_program(g, core, T, topo):
+    plan = make_plan(T, topo)
+    land, sem, off = T.land, T.sem, plan["off"]
+    rank = T.rank_of(core)
+
+    if core == plan["root"]:
+        c0, c1 = off[rank], off[rank + 1]
+        g.scalar.dma_start(T.y[:, c0:c1], T.x[:, 0:c1 - c0]).then_inc(sem.stored, 16)
+        queues = [g.sync, g.scalar]
+        for i, s in enumerate(plan["stores"]):
+            q = queues[i % 2]
+            q.wait_ge(sem[s["sem"]], s["count"])
+            q.dma_start(T.y[:, s["c0"]:s["c1"]], land[:, s["c0"]:s["c1"]]).then_inc(sem.stored, 16)
+        g.wait_ge(sem.stored, 16 * (len(plan["stores"]) + 1))
+        return
+
+    if rank is not None:
+        g.sync.dma_start(land[:, off[rank]:off[rank + 1]], T.x[:, 0:plan["widths"][rank]]).then_inc(sem.loaded, 16)
+        g.wait_ge(sem.loaded, 16)
+
+    sent = 0
+    for s in plan["sends"].get(core, []):
+        if s["wait"] is not None:
+            g.wait_ge(sem[s["wait"][0]], s["wait"][1])
+        rid, pid, _se = topo.addr(s["dst"])
+        piece = land[:, s["c0"]:s["c1"]]
+        g.remote_dma(piece, piece, sem[s["sem"]], sem.sent, pid, rid, topo.mask(core, s["dst"]))
+        sent += engines(topo, core, s["dst"])
+    if sent:
+        g.wait_ge(sem.sent, sent)

@@ -1,5 +1,6 @@
 TOTAL = 2374
 MIN_STORE = 64
+NARROW = 16
 N_IN = 4
 N_ARR = 8
 
@@ -9,81 +10,157 @@ SCRATCH = {
 SEMAPHORES = ["loaded", "sent", "stored"] + ["in%d" % k for k in range(N_IN)] + ["a%d" % k for k in range(N_ARR)]
 
 
-def engines(topo, src, dst):
-    return bin(topo.mask(src, dst)).count("1")
-
-
-def make_plan(T, topo):
+def route_pieces(T, topo):
     widths = T.tables["WIDTHS"]
     cores = list(T.cores)
     root_rank = T.root if T.root is not None else 0
     root = cores[root_rank]
     off = [sum(widths[:r]) for r in range(len(widths) + 1)]
     others = [r for r in range(len(cores)) if r != root_rank]
+    root_chip = topo.chip(root)
+    mate_chip = root_chip ^ 1
+    chip_of = {r: topo.chip(cores[r]) for r in others}
+    die_of = {r: topo.die(cores[r]) for r in others}
+    plane = [r for r in others if chip_of[r] != root_chip and (chip_of[r] & 1) == (root_chip & 1)]
+    far = [r for r in others if chip_of[r] != mate_chip and (chip_of[r] & 1) != (root_chip & 1)]
+
+    def neighbour(r):
+        for n in (r + 1, r - 1):
+            if n in others and chip_of[n] == chip_of[r] and die_of[n] != die_of[r]:
+                return n
+        return None
+
+    lo = {r: off[r] for r in others}
+    hi = {r: off[r + 1] for r in others}
+    way = {}
+    pieces = []
+
+    switch = {0: 0, 1: 0}
+    for r in others:
+        if chip_of[r] == root_chip:
+            way[r] = (cores[r], root)
+    for r in plane:
+        n = neighbour(r)
+        if widths[r] < NARROW and n is not None and widths[n] >= NARROW:
+            way[r] = (cores[r], cores[n], root)
+            switch[die_of[n]] += widths[r]
+        else:
+            way[r] = (cores[r], root)
+            switch[die_of[r]] += widths[r]
+
+    for d in (0, 1):
+        enter = sum(widths[r] for r in far if die_of[r] == d)
+        able = [r for r in far if die_of[r] == d and topo.may_write(cores[r], root)]
+        e = max(0, -((sum(switch.values()) - 2 * enter) // 3))
+        if able and e:
+            m = max(able, key=lambda r: (widths[r], r))
+            e = min(e, widths[m] - 1)
+            hi[m] -= e
+            pieces.append((hi[m], hi[m] + e, m, (cores[m], root)))
+            switch[d] += e
+
+    heavy = max((0, 1), key=lambda d: switch[d])
+    move = (switch[heavy] - switch[1 - heavy]) // 2
+    able = [r for r in plane if die_of[r] == heavy and len(way[r]) == 2 and widths[r] > move
+            and neighbour(r) is not None and len(way[neighbour(r)]) == 2]
+    if able and move:
+        m = min(able, key=lambda r: (widths[neighbour(r)], -r))
+        n = neighbour(m)
+        if n > m:
+            hi[m] -= move
+            cut = (hi[m], hi[m] + move)
+        else:
+            cut = (lo[m], lo[m] + move)
+            lo[m] += move
+        pieces.append((cut[0], cut[1], m, (cores[m], cores[n], root)))
+
+    relays = [c for c in range(mate_chip * 8, mate_chip * 8 + 8) if topo.may_write(c, root)]
+    die_load = {0: 0, 1: 0}
+    core_load = {c: 0 for c in relays}
+    todo = []
+    for r in others:
+        if r in way:
+            continue
+        if cores[r] in relays:
+            way[r] = (cores[r], root)
+            die_load[die_of[r]] += hi[r] - lo[r]
+            core_load[cores[r]] += hi[r] - lo[r]
+        else:
+            todo.append(r)
+    for r in sorted(todo, key=lambda q: (lo[q] - hi[q], q)):
+        c = min(relays, key=lambda k: (die_load[topo.die(k)], core_load[k], k))
+        way[r] = (cores[r], c, root)
+        die_load[topo.die(c)] += hi[r] - lo[r]
+        core_load[c] += hi[r] - lo[r]
+
+    pieces += [(lo[r], hi[r], r, way[r]) for r in others]
+    return sorted(pieces), off, root, others
+
+
+def make_plan(T, topo):
+    pieces, off, root, others = route_pieces(T, topo)
+    widths = T.tables["WIDTHS"]
+    cores = list(T.cores)
 
     blocks = []
     for r in others:
         new_chip = not blocks or topo.chip(cores[blocks[-1][-1]]) != topo.chip(cores[r])
         adjacent = bool(blocks) and blocks[-1][-1] == r - 1
         chip_width = sum(widths[q] for q in others if topo.chip(cores[q]) == topo.chip(cores[r]))
-        if blocks and adjacent and (not new_chip or chip_width < MIN_STORE):
+        if adjacent and (not new_chip or chip_width < MIN_STORE):
             blocks[-1].append(r)
         else:
             blocks.append([r])
     block_of = {r: b for b, rs in enumerate(blocks) for r in rs}
 
-    mate_chip = topo.chip(root) ^ 1
-    relays = [c for c in range(mate_chip * 8, mate_chip * 8 + 8) if topo.may_write(c, root)]
-    die_load = {0: 0, 1: 0}
-    core_load = {c: 0 for c in relays}
-    holder = {}
-    relayed = []
-    for r in others:
-        c = cores[r]
-        same_parity = (topo.chip(c) & 1) == (topo.chip(root) & 1)
-        if same_parity or (topo.chip(c) == mate_chip and topo.may_write(c, root)):
-            holder[r] = c
-            if not same_parity:
-                die_load[topo.die(c)] += widths[r]
-                core_load[c] += widths[r]
-        else:
-            relayed.append(r)
-    for r in sorted(relayed, key=lambda q: (-widths[q], q)):
-        c = min(relays, key=lambda k: (die_load[topo.die(k)], core_load[k], k))
-        holder[r] = c
-        die_load[topo.die(c)] += widths[r]
-        core_load[c] += widths[r]
+    writes = {}
+    for h in sorted({c for p in pieces for c in p[3][:-1]}):
+        ws = []
+        for c0, c1, r, path in pieces:
+            if h not in path[:-1]:
+                continue
+            ahead = path[path.index(h):]
+            guest = path[0] != h
+            if ws and ws[-1]["c1"] == c0 and ws[-1]["ahead"] == ahead and ws[-1]["block"] == block_of[r]:
+                ws[-1]["c1"] = c1
+                ws[-1]["guest"] = ws[-1]["guest"] or guest
+            else:
+                ws.append({"c0": c0, "c1": c1, "ahead": ahead, "block": block_of[r], "guest": guest, "count": 0})
+        ws.sort(key=lambda w: (w["guest"], 0 if w["guest"] else -len(w["ahead"]), w["c1"] - w["c0"], w["c0"]))
+        leaves = any(topo.chip(w["ahead"][1]) != topo.chip(h) for w in ws)
+        k = 0
+        for w in ws:
+            w["dst"] = w["ahead"][1]
+            w["mask"] = topo.mask(h, w["dst"])
+            if leaves and topo.chip(w["dst"]) == topo.chip(h):
+                w["mask"] = 0xFF00
+            w["engines"] = bin(w["mask"]).count("1")
+            if w["guest"]:
+                w["wait"] = "in%d" % k
+                k += 1
+        assert k <= N_IN
+        writes[h] = ws
 
-    sends = {}
     arrive = [0] * len(blocks)
     depth = [1] * len(blocks)
-    for h in sorted(set(holder.values())):
-        groups = []
-        for r in sorted(q for q in others if holder[q] == h):
-            if groups and groups[-1][-1] == r - 1 and block_of[groups[-1][-1]] == block_of[r]:
-                groups[-1].append(r)
+    for h, ws in writes.items():
+        for w in ws:
+            if w["dst"] == root:
+                w["sem"] = "a%d" % w["block"]
+                arrive[w["block"]] += w["engines"]
+                if w["guest"]:
+                    depth[w["block"]] = 2
             else:
-                groups.append([r])
-        groups.sort(key=lambda rs: (off[rs[-1] + 1] - off[rs[0]], rs[0]))
-        k = 0
-        for rs in groups:
-            guests = [r for r in rs if cores[r] != h]
-            wait = None
-            if guests:
-                wait = ("in%d" % k, sum(engines(topo, cores[r], h) for r in guests))
-                for r in guests:
-                    sends.setdefault(cores[r], []).append(
-                        {"c0": off[r], "c1": off[r + 1], "dst": h, "sem": "in%d" % k, "wait": None})
-                k += 1
-                depth[block_of[rs[0]]] = 2
-            sends.setdefault(h, []).append(
-                {"c0": off[rs[0]], "c1": off[rs[-1] + 1], "dst": root, "sem": "a%d" % block_of[rs[0]], "wait": wait})
-            arrive[block_of[rs[0]]] += engines(topo, h, root)
+                nxt = [v for v in writes[w["dst"]] if v["c0"] <= w["c0"] and w["c1"] <= v["c1"]]
+                assert len(nxt) == 1 and nxt[0]["guest"]
+                w["sem"] = nxt[0]["wait"]
+                nxt[0]["count"] += w["engines"]
+    assert len(blocks) <= N_ARR
 
     stores = [{"c0": off[rs[0]], "c1": off[rs[-1] + 1], "sem": "a%d" % b, "count": arrive[b], "depth": depth[b]}
               for b, rs in enumerate(blocks)]
     stores.sort(key=lambda s: (s["depth"], s["c1"] - s["c0"], s["c0"]))
-    return {"root": root, "root_rank": root_rank, "off": off, "widths": widths, "sends": sends, "stores": stores}
+    return {"root": root, "off": off, "widths": widths, "writes": writes, "stores": stores}
 
 
 def rank_program(g, core, T, topo):
@@ -107,12 +184,12 @@ def rank_program(g, core, T, topo):
         g.wait_ge(sem.loaded, 16)
 
     sent = 0
-    for s in plan["sends"].get(core, []):
-        if s["wait"] is not None:
-            g.wait_ge(sem[s["wait"][0]], s["wait"][1])
-        rid, pid, _se = topo.addr(s["dst"])
-        piece = land[:, s["c0"]:s["c1"]]
-        g.remote_dma(piece, piece, sem[s["sem"]], sem.sent, pid, rid, topo.mask(core, s["dst"]))
-        sent += engines(topo, core, s["dst"])
+    for w in plan["writes"].get(core, []):
+        if w["guest"]:
+            g.wait_ge(sem[w["wait"]], w["count"])
+        rid, pid, _se = topo.addr(w["dst"])
+        piece = land[:, w["c0"]:w["c1"]]
+        g.remote_dma(piece, piece, sem[w["sem"]], sem.sent, pid, rid, w["mask"])
+        sent += w["engines"]
     if sent:
         g.wait_ge(sem.sent, sent)

TOTAL = 2374
MIN_STORE = 64
NARROW = 16
N_IN = 4
N_ARR = 8

SCRATCH = {
    "land": ("sbuf", [128, TOTAL], "float32"),
}
SEMAPHORES = ["loaded", "sent", "stored"] + ["in%d" % k for k in range(N_IN)] + ["a%d" % k for k in range(N_ARR)]


def route_pieces(T, topo):
    widths = T.tables["WIDTHS"]
    cores = list(T.cores)
    root_rank = T.root if T.root is not None else 0
    root = cores[root_rank]
    off = [sum(widths[:r]) for r in range(len(widths) + 1)]
    others = [r for r in range(len(cores)) if r != root_rank]
    root_chip = topo.chip(root)
    mate_chip = root_chip ^ 1
    chip_of = {r: topo.chip(cores[r]) for r in others}
    die_of = {r: topo.die(cores[r]) for r in others}
    plane = [r for r in others if chip_of[r] != root_chip and (chip_of[r] & 1) == (root_chip & 1)]
    far = [r for r in others if chip_of[r] != mate_chip and (chip_of[r] & 1) != (root_chip & 1)]

    def neighbour(r):
        for n in (r + 1, r - 1):
            if n in others and chip_of[n] == chip_of[r] and die_of[n] != die_of[r]:
                return n
        return None

    lo = {r: off[r] for r in others}
    hi = {r: off[r + 1] for r in others}
    way = {}
    pieces = []

    switch = {0: 0, 1: 0}
    for r in others:
        if chip_of[r] == root_chip:
            way[r] = (cores[r], root)
    for r in plane:
        n = neighbour(r)
        if widths[r] < NARROW and n is not None and widths[n] >= NARROW:
            way[r] = (cores[r], cores[n], root)
            switch[die_of[n]] += widths[r]
        else:
            way[r] = (cores[r], root)
            switch[die_of[r]] += widths[r]

    for d in (0, 1):
        enter = sum(widths[r] for r in far if die_of[r] == d)
        able = [r for r in far if die_of[r] == d and topo.may_write(cores[r], root)]
        e = max(0, -((sum(switch.values()) - 2 * enter) // 3))
        if able and e:
            m = max(able, key=lambda r: (widths[r], r))
            e = min(e, widths[m] - 1)
            hi[m] -= e
            pieces.append((hi[m], hi[m] + e, m, (cores[m], root)))
            switch[d] += e

    heavy = max((0, 1), key=lambda d: switch[d])
    move = (switch[heavy] - switch[1 - heavy]) // 2
    able = [r for r in plane if die_of[r] == heavy and len(way[r]) == 2 and widths[r] > move
            and neighbour(r) is not None and len(way[neighbour(r)]) == 2]
    if able and move:
        m = min(able, key=lambda r: (widths[neighbour(r)], -r))
        n = neighbour(m)
        if n > m:
            hi[m] -= move
            cut = (hi[m], hi[m] + move)
        else:
            cut = (lo[m], lo[m] + move)
            lo[m] += move
        pieces.append((cut[0], cut[1], m, (cores[m], cores[n], root)))

    relays = [c for c in range(mate_chip * 8, mate_chip * 8 + 8) if topo.may_write(c, root)]
    die_load = {0: 0, 1: 0}
    core_load = {c: 0 for c in relays}
    todo = []
    for r in others:
        if r in way:
            continue
        if cores[r] in relays:
            way[r] = (cores[r], root)
            die_load[die_of[r]] += hi[r] - lo[r]
            core_load[cores[r]] += hi[r] - lo[r]
        else:
            todo.append(r)
    for r in sorted(todo, key=lambda q: (lo[q] - hi[q], q)):
        c = min(relays, key=lambda k: (die_load[topo.die(k)], core_load[k], k))
        way[r] = (cores[r], c, root)
        die_load[topo.die(c)] += hi[r] - lo[r]
        core_load[c] += hi[r] - lo[r]

    pieces += [(lo[r], hi[r], r, way[r]) for r in others]
    return sorted(pieces), off, root, others


def make_plan(T, topo):
    pieces, off, root, others = route_pieces(T, topo)
    widths = T.tables["WIDTHS"]
    cores = list(T.cores)

    blocks = []
    for r in others:
        new_chip = not blocks or topo.chip(cores[blocks[-1][-1]]) != topo.chip(cores[r])
        adjacent = bool(blocks) and blocks[-1][-1] == r - 1
        chip_width = sum(widths[q] for q in others if topo.chip(cores[q]) == topo.chip(cores[r]))
        if adjacent and (not new_chip or chip_width < MIN_STORE):
            blocks[-1].append(r)
        else:
            blocks.append([r])
    block_of = {r: b for b, rs in enumerate(blocks) for r in rs}

    writes = {}
    for h in sorted({c for p in pieces for c in p[3][:-1]}):
        ws = []
        for c0, c1, r, path in pieces:
            if h not in path[:-1]:
                continue
            ahead = path[path.index(h):]
            guest = path[0] != h
            if ws and ws[-1]["c1"] == c0 and ws[-1]["ahead"] == ahead and ws[-1]["block"] == block_of[r]:
                ws[-1]["c1"] = c1
                ws[-1]["guest"] = ws[-1]["guest"] or guest
            else:
                ws.append({"c0": c0, "c1": c1, "ahead": ahead, "block": block_of[r], "guest": guest, "count": 0})
        ws.sort(key=lambda w: (w["guest"], 0 if w["guest"] else -len(w["ahead"]), w["c1"] - w["c0"], w["c0"]))
        leaves = any(topo.chip(w["ahead"][1]) != topo.chip(h) for w in ws)
        k = 0
        for w in ws:
            w["dst"] = w["ahead"][1]
            w["mask"] = topo.mask(h, w["dst"])
            if leaves and topo.chip(w["dst"]) == topo.chip(h):
                w["mask"] = 0xFF00
            w["engines"] = bin(w["mask"]).count("1")
            if w["guest"]:
                w["wait"] = "in%d" % k
                k += 1
        assert k <= N_IN
        writes[h] = ws

    arrive = [0] * len(blocks)
    depth = [1] * len(blocks)
    for h, ws in writes.items():
        for w in ws:
            if w["dst"] == root:
                w["sem"] = "a%d" % w["block"]
                arrive[w["block"]] += w["engines"]
                if w["guest"]:
                    depth[w["block"]] = 2
            else:
                nxt = [v for v in writes[w["dst"]] if v["c0"] <= w["c0"] and w["c1"] <= v["c1"]]
                assert len(nxt) == 1 and nxt[0]["guest"]
                w["sem"] = nxt[0]["wait"]
                nxt[0]["count"] += w["engines"]
    assert len(blocks) <= N_ARR

    stores = [{"c0": off[rs[0]], "c1": off[rs[-1] + 1], "sem": "a%d" % b, "count": arrive[b], "depth": depth[b]}
              for b, rs in enumerate(blocks)]
    stores.sort(key=lambda s: (s["depth"], s["c1"] - s["c0"], s["c0"]))
    return {"root": root, "off": off, "widths": widths, "writes": writes, "stores": stores}


def rank_program(g, core, T, topo):
    plan = make_plan(T, topo)
    land, sem, off = T.land, T.sem, plan["off"]
    rank = T.rank_of(core)

    if core == plan["root"]:
        c0, c1 = off[rank], off[rank + 1]
        g.scalar.dma_start(T.y[:, c0:c1], T.x[:, 0:c1 - c0]).then_inc(sem.stored, 16)
        queues = [g.sync, g.scalar]
        for i, s in enumerate(plan["stores"]):
            q = queues[i % 2]
            q.wait_ge(sem[s["sem"]], s["count"])
            q.dma_start(T.y[:, s["c0"]:s["c1"]], land[:, s["c0"]:s["c1"]]).then_inc(sem.stored, 16)
        g.wait_ge(sem.stored, 16 * (len(plan["stores"]) + 1))
        return

    if rank is not None:
        g.sync.dma_start(land[:, off[rank]:off[rank + 1]], T.x[:, 0:plan["widths"][rank]]).then_inc(sem.loaded, 16)
        g.wait_ge(sem.loaded, 16)

    sent = 0
    for w in plan["writes"].get(core, []):
        if w["guest"]:
            g.wait_ge(sem[w["wait"]], w["count"])
        rid, pid, _se = topo.addr(w["dst"])
        piece = land[:, w["c0"]:w["c1"]]
        g.remote_dma(piece, piece, sem[w["sem"]], sem.sent, pid, rid, w["mask"])
        sent += w["engines"]
    if sent:
        g.wait_ge(sem.sent, sent)
